import numpy as np
import ml_dtypes


def mxq(x, axis, fmt="e4m3"):
    dtype, down = {"e4m3": (ml_dtypes.float8_e4m3fn, 7), "e5m2": (ml_dtypes.float8_e5m2, 14)}[fmt]
    v = np.moveaxis(np.asarray(x, np.float32).astype(ml_dtypes.bfloat16).astype(np.float64), axis, -1)
    blocks = v.reshape(v.shape[:-1] + (-1, 32))
    amax = np.abs(blocks).max(-1, keepdims=True)
    byte = np.maximum(np.where(amax > 0, np.frexp(amax)[1] - 1 + 127, 0) - down, 1)
    scale = np.exp2(byte - 127.0)
    codes = (blocks / scale).astype(np.float32).astype(dtype).astype(np.float64)
    return np.moveaxis((codes * scale).reshape(v.shape), -1, axis)


WIDE = False


def mx_kscale(k, group=512):
    if not WIDE:
        return np.ones(k)
    levels = np.array([18, -18])
    if group != 512:
        return np.exp2(np.random.permutation(np.resize(levels, k // group))).repeat(group)
    if k % 512:
        return np.exp2(np.random.permutation(np.resize(levels, k // 32))).repeat(32)
    a = np.empty((k // 512, 16))
    for p in range(k // 512):
        a[p, :8] = np.random.permutation(np.resize(levels, 8))
        for g in range(8):
            far = levels[np.abs(levels - a[p, g]) >= 10]
            a[p, g + 8] = far[np.random.randint(len(far))]
    return np.exp2(a.ravel()).repeat(32)


def f64(x):
    return np.asarray(x).astype(np.float64)


G, D, M, N = 4, 128, 128, 512


def setup_inputs():
    n = np.random.standard_normal
    s_d = mx_kscale(D, 0)
    return {
        "x": (n((G, D, N)) * s_d[:, None]).astype(np.float32),
        "w1": (n((G, D, M)) / np.sqrt(D) / s_d[:, None]).astype(np.float32),
        "w2": (n((G, D, M)) / np.sqrt(D) / s_d[:, None]).astype(np.float32),
        "ra": (np.random.uniform(0.3, 1.5, (G, M, 1))).astype(np.float32),
        "dx": (n((G, D, N)) * s_d[:, None]).astype(np.float32),
        "og": (np.random.uniform(0.5, 2.0, (G, M, 1))).astype(np.float32),
        "base": (0.3 * n((G, M, N))).astype(np.float32),
    }


def reference(x, w1, w2, ra, dx, og, base):
    w1q = mxq(f64(w1), 1, "e4m3")
    xq = mxq(f64(x), 1, "e4m3")
    z1 = w1q.transpose(0, 2, 1) @ xq
    dxq = mxq(f64(dx), 1, "e4m3")
    tz1 = w1q.transpose(0, 2, 1) @ dxq
    w2q = mxq(f64(w2), 1, "e4m3")
    z2 = w2q.transpose(0, 2, 1) @ xq
    tz2 = w2q.transpose(0, 2, 1) @ dxq
    nn = np.sqrt(np.square(z1) + np.square(z2) + f64(ra))
    xnn = (tz1 * z1 * 2.0 + tz2 * z2 * 2.0) * 0.5 / nn
    xh = (tz1 - xnn * z1 / nn) / nn
    y = xh * f64(og) + f64(base)
    return y

@@ -1,0 +1,232 @@
+from contextlib import ExitStack
+
+import concourse.mybir as mybir
+
+G, D, M, N = 4, 128, 128, 512
+FLOPS = 4 * 2 * G * D * M * N
+
+F32 = mybir.dt.float32
+BF16 = mybir.dt.bfloat16
+U32 = mybir.dt.uint32
+U8 = mybir.dt.uint8
+FP8X4 = mybir.dt.float8_e4m3fn_x4
+ACT = mybir.ActivationFunctionType
+ALU = mybir.AluOpType
+
+P = 128
+PACK = 4
+ROWS = D // PACK
+RUN = 4
+MM_N = 128
+BANK = 512
+CHUNKS = [(0, 128), (128, 128), (256, 256)]
+LAST_DX_VECTOR_COLS = 128
+
+
+def tile_rows_tnsphere_kernel(tc, x, w1, w2, ra, dx, og, base, out):
+    nc = tc.nc
+
+    with ExitStack() as ctx:
+        sb = ctx.enter_context(tc.tile_pool(name="sb", bufs=1))
+        psum = ctx.enter_context(tc.psum_pool(name="psum", bufs=1))
+        ctx.enter_context(tc.manual_schedule())
+
+        def operand(name, width):
+            return {
+                "raw": sb.tile([P, PACK, width], F32, name=name + "_raw", align_bytes=64),
+                "rounded": sb.tile([P, width * PACK], BF16, name=name + "_rounded", align_bytes=64),
+                "codes": sb.tile([P, width], U32, name=name + "_codes", align_bytes=64),
+                "scales": sb.tile([P, width], U8, name=name + "_scales", align_bytes=64),
+                "width": width,
+            }
+
+        def load(op, src, c0):
+            rows = src.rearrange("g (p j) n -> (g p) j n", j=PACK)
+            nc.sync.dma_start(out=op["raw"][:], in_=rows[:, :, c0 : c0 + op["width"]])
+
+        def round_views(op, c0, c1):
+            dst = op["rounded"][:, c0 * PACK : c1 * PACK].rearrange("p (c i j) -> p c j i", i=RUN, j=PACK)
+            src = op["raw"][:, :, c0:c1].rearrange("p j (c i) -> p c j i", i=RUN)
+            return dst, src
+
+        def round_on_vector(op, c0, c1):
+            dst, src = round_views(op, c0, c1)
+            nc.vector.tensor_copy(out=dst, in_=src)
+
+        def round_on_scalar(op, c0, c1):
+            dst, src = round_views(op, c0, c1)
+            nc.scalar.copy(out=dst, in_=src)
+
+        def quantize(op):
+            nc.vector.quantize_mx(out=op["codes"][:].bitcast(FP8X4), scales=op["scales"][:], in_=op["rounded"][:])
+
+        def products(bank, g, moving):
+            rows = slice(ROWS * g, ROWS * (g + 1))
+            width = moving["width"]
+            for half, w in enumerate((w1_op, w2_op)):
+                for c in range(0, width, MM_N):
+                    nc.tensor.matmul_mx(
+                        out=bank[:, half * width + c : half * width + c + MM_N],
+                        lhsT=w["codes"][rows, :].bitcast(FP8X4),
+                        lhsT_scale=w["scales"][rows, :],
+                        rhs=moving["codes"][rows, c : c + MM_N].bitcast(FP8X4),
+                        rhs_scale=moving["scales"][rows, c : c + MM_N],
+                        start=True,
+                        stop=True,
+                    )
+
+        w1_op = operand("w1", M)
+        w2_op = operand("w2", M)
+        x_ops = [operand("x%d" % k, width) for k, (c0, width) in enumerate(CHUNKS)]
+        dx_ops = [operand("dx%d" % k, width) for k, (c0, width) in enumerate(CHUNKS)]
+        z_banks = [psum.tile([P, BANK], F32, name="z%d" % g) for g in range(G)]
+        tz_banks = [psum.tile([P, BANK], F32, name="tz%d" % g) for g in range(G)]
+
+        def per_chunk(name, parts):
+            return [sb.tile([P, G, parts * width], F32, name="%s%d" % (name, k)) for k, (c0, width) in enumerate(CHUNKS)]
+
+        squares = per_chunk("squares", 2)
+        z1 = per_chunk("z1", 1)
+        term1 = per_chunk("term1", 1)
+        z12 = per_chunk("z12", 1)
+        term2 = per_chunk("term2", 1)
+        sumsq = sb.tile([P, G, N], F32)
+        numer = sb.tile([P, G, N], F32)
+        logs = sb.tile([P, G, N], F32)
+        inv_cube = sb.tile([P, G, N], F32)
+        xh = sb.tile([P, G, N], F32)
+        result = sb.tile([P, G, N], F32)
+        base_sb = sb.tile([P, G, N], F32)
+        params_rows = sb.tile([P, P], F32, align_bytes=64)
+        params = sb.tile([P, P], F32, align_bytes=64)
+        inv_ra = sb.tile([P, G], F32)
+        ln_ra = sb.tile([P, G], F32)
+        exp_bias = sb.tile([P, G], F32)
+
+        load(w1_op, w1, 0)
+        load(w2_op, w2, 0)
+        load(x_ops[0], x, CHUNKS[0][0])
+        load(dx_ops[0], dx, CHUNKS[0][0])
+        load(x_ops[1], x, CHUNKS[1][0])
+        load(x_ops[2], x, CHUNKS[2][0])
+        load(dx_ops[1], dx, CHUNKS[1][0])
+        load(dx_ops[2], dx, CHUNKS[2][0])
+        nc.sync.dma_start(out=base_sb[:], in_=base.rearrange("g m n -> m g n"))
+
+        nc.vector.memset(params_rows[:], 0.0)
+        for r, vec in enumerate((ra, og)):
+            nc.scalar.dma_start(
+                out=params_rows[r:P:32, :].rearrange("q (g c) -> q g c", g=G),
+                in_=vec.rearrange("g (q c) o -> q g (c o)", c=32),
+            )
+        ra_cols = params[:, 0:P:32]
+
+        round_on_vector(w1_op, 0, M)
+        nc.vector.transpose(out=params[:], in_=params_rows[:])
+        quantize(w1_op)
+        round_on_vector(w2_op, 0, M)
+        nc.vector.reciprocal(out=inv_ra[:], in_=ra_cols)
+        quantize(w2_op)
+        nc.scalar.activation(out=ln_ra[:], in_=ra_cols, func=ACT.Ln)
+        nc.scalar.mul(out=exp_bias[:], in_=ln_ra[:], mul=-1.5)
+
+        round_on_vector(x_ops[0], 0, x_ops[0]["width"])
+        quantize(x_ops[0])
+        for g in range(G):
+            products(z_banks[g], g, x_ops[0])
+        round_on_vector(dx_ops[0], 0, dx_ops[0]["width"])
+        quantize(dx_ops[0])
+        for g in range(G):
+            products(tz_banks[g], g, dx_ops[0])
+        round_on_vector(x_ops[1], 0, x_ops[1]["width"])
+
+        def square_step(k, g):
+            width = CHUNKS[k][1]
+            nc.scalar.activation(out=squares[k][:, g, :], in_=z_banks[g][:, 0 : 2 * width], func=ACT.Square)
+
+        def copy_step(k, g):
+            width = CHUNKS[k][1]
+            nc.scalar.copy(out=z1[k][:, g, :], in_=z_banks[g][:, 0:width])
+
+        def term1_step(k, g):
+            width = CHUNKS[k][1]
+            nc.vector.scalar_tensor_tensor(
+                out=term1[k][:, g, :], in0=squares[k][:, g, width : 2 * width], scalar=params[:, 32 * g : 32 * g + 1],
+                in1=tz_banks[g][:, 0:width], op0=ALU.add, op1=ALU.mult,
+            )
+
+        def z12_step(k, g):
+            width = CHUNKS[k][1]
+            nc.vector.tensor_tensor(out=z12[k][:, g, :], in0=z1[k][:, g, :], in1=z_banks[g][:, width : 2 * width], op=ALU.mult)
+
+        def term2_step(k, g):
+            width = CHUNKS[k][1]
+            nc.vector.tensor_tensor(out=term2[k][:, g, :], in0=z12[k][:, g, :], in1=tz_banks[g][:, width : 2 * width], op=ALU.mult)
+
+        def sumsq_step(k):
+            c0, width = CHUNKS[k]
+            nc.vector.tensor_tensor(
+                out=sumsq[:, :, c0 : c0 + width], in0=squares[k][:, :, 0:width], in1=squares[k][:, :, width : 2 * width], op=ALU.add
+            )
+
+        def numer_step(k):
+            c0, width = CHUNKS[k]
+            nc.vector.tensor_tensor(out=numer[:, :, c0 : c0 + width], in0=term1[k][:], in1=term2[k][:], op=ALU.subtract)
+
+        def early_chunk(k, after_first_term):
+            for g in range(G):
+                square_step(k, g)
+                copy_step(k, g)
+                term1_step(k, g)
+                if g == 0:
+                    after_first_term()
+                else:
+                    term2_step(k, g - 1)
+                z12_step(k, g)
+                products(z_banks[g], g, x_ops[k + 1])
+            sumsq_step(k)
+            term2_step(k, G - 1)
+
+        early_chunk(0, lambda: quantize(x_ops[1]))
+        round_on_scalar(x_ops[2], 0, x_ops[2]["width"])
+        round_on_vector(dx_ops[1], 0, dx_ops[1]["width"])
+        numer_step(0)
+        quantize(dx_ops[1])
+        for g in range(G):
+            products(tz_banks[g], g, dx_ops[1])
+
+        early_chunk(1, lambda: quantize(x_ops[2]))
+        round_on_scalar(dx_ops[2], LAST_DX_VECTOR_COLS, dx_ops[2]["width"])
+        round_on_vector(dx_ops[2], 0, LAST_DX_VECTOR_COLS)
+        numer_step(1)
+        quantize(dx_ops[2])
+        for g in range(G):
+            products(tz_banks[g], g, dx_ops[2])
+
+        for g in range(G):
+            square_step(2, g)
+            term1_step(2, g)
+        sumsq_step(2)
+        for g in range(G):
+            copy_step(2, g)
+        for g in range(G):
+            nc.scalar.activation(out=logs[:, g, :], in_=sumsq[:, g, :], func=ACT.Ln, scale=inv_ra[:, g : g + 1], bias=1.0)
+        for g in range(G):
+            z12_step(2, g)
+        for g in range(G):
+            term2_step(2, g)
+        numer_step(2)
+
+        def xh_step(g):
+            nc.scalar.activation(out=inv_cube[:, g, :], in_=logs[:, g, :], func=ACT.Exp, scale=-1.5, bias=exp_bias[:, g : g + 1])
+            nc.vector.tensor_tensor(out=xh[:, g, :], in0=numer[:, g, :], in1=inv_cube[:, g, :], op=ALU.mult)
+
+        xh_step(0)
+        for g in range(G):
+            if g + 1 < G:
+                xh_step(g + 1)
+            nc.vector.scalar_tensor_tensor(
+                out=result[:, g, :], in0=xh[:, g, :], scalar=params[:, 32 * g + 1 : 32 * g + 2],
+                in1=base_sb[:, g, :], op0=ALU.mult, op1=ALU.add,
+            )
+            nc.sync.dma_start(out=out[g], in_=result[:, g, :])

@@ -17,10 +17,9 @@ P = 128
 PACK = 4
 ROWS = D // PACK
 RUN = 4
-MM_N = 128
-BANK = 512
-CHUNKS = [(0, 128), (128, 128), (256, 256)]
-LAST_DX_VECTOR_COLS = 128
+X_PIECES = [(0, 256), (256, 256)]
+DX_PIECES = [(0, 256), (256, 256)]
+LAST_X_VECTOR_COLS = 160
 
 
 def tile_rows_tnsphere_kernel(tc, x, w1, w2, ra, dx, og, base, out):
@@ -31,202 +30,184 @@ def tile_rows_tnsphere_kernel(tc, x, w1, w2, ra, dx, og, base, out):
         psum = ctx.enter_context(tc.psum_pool(name="psum", bufs=1))
         ctx.enter_context(tc.manual_schedule())
 
-        def operand(name, width):
+        def operand(name, src, pieces):
+            width = sum(w for c0, w in pieces)
             return {
-                "raw": sb.tile([P, PACK, width], F32, name=name + "_raw", align_bytes=64),
-                "rounded": sb.tile([P, width * PACK], BF16, name=name + "_rounded", align_bytes=64),
+                "rows": src.rearrange("g (p j) n -> (g p) j n", j=PACK),
+                "pieces": pieces,
+                "raw": [sb.tile([P, PACK, w], F32, name="%s_raw%d" % (name, c0), align_bytes=64) for c0, w in pieces],
+                "rounded": [sb.tile([P, w * PACK], BF16, name="%s_rounded%d" % (name, c0), align_bytes=64) for c0, w in pieces],
                 "codes": sb.tile([P, width], U32, name=name + "_codes", align_bytes=64),
                 "scales": sb.tile([P, width], U8, name=name + "_scales", align_bytes=64),
-                "width": width,
             }
 
-        def load(op, src, c0):
-            rows = src.rearrange("g (p j) n -> (g p) j n", j=PACK)
-            nc.sync.dma_start(out=op["raw"][:], in_=rows[:, :, c0 : c0 + op["width"]])
+        def load(op, k):
+            c0, w = op["pieces"][k]
+            nc.sync.dma_start(out=op["raw"][k][:], in_=op["rows"][:, :, c0 : c0 + w])
 
-        def round_views(op, c0, c1):
-            dst = op["rounded"][:, c0 * PACK : c1 * PACK].rearrange("p (c i j) -> p c j i", i=RUN, j=PACK)
-            src = op["raw"][:, :, c0:c1].rearrange("p j (c i) -> p c j i", i=RUN)
+        def round_views(op, k, c0, c1):
+            dst = op["rounded"][k][:, c0 * PACK : c1 * PACK].rearrange("p (c i j) -> p c j i", i=RUN, j=PACK)
+            src = op["raw"][k][:, :, c0:c1].rearrange("p j (c i) -> p c j i", i=RUN)
             return dst, src
 
-        def round_on_vector(op, c0, c1):
-            dst, src = round_views(op, c0, c1)
+        def round_on_vector(op, k, c0, c1):
+            dst, src = round_views(op, k, c0, c1)
             nc.vector.tensor_copy(out=dst, in_=src)
 
-        def round_on_scalar(op, c0, c1):
-            dst, src = round_views(op, c0, c1)
+        def round_on_scalar(op, k, c0, c1):
+            dst, src = round_views(op, k, c0, c1)
             nc.scalar.copy(out=dst, in_=src)
 
-        def quantize(op):
-            nc.vector.quantize_mx(out=op["codes"][:].bitcast(FP8X4), scales=op["scales"][:], in_=op["rounded"][:])
+        def quantize(op, k):
+            c0, w = op["pieces"][k]
+            nc.vector.quantize_mx(
+                out=op["codes"][:, c0 : c0 + w].bitcast(FP8X4), scales=op["scales"][:, c0 : c0 + w], in_=op["rounded"][k][:]
+            )
 
-        def products(bank, g, moving):
+        def product(bank, g, weights, moving):
             rows = slice(ROWS * g, ROWS * (g + 1))
-            width = moving["width"]
-            for half, w in enumerate((w1_op, w2_op)):
-                for c in range(0, width, MM_N):
-                    nc.tensor.matmul_mx(
-                        out=bank[:, half * width + c : half * width + c + MM_N],
-                        lhsT=w["codes"][rows, :].bitcast(FP8X4),
-                        lhsT_scale=w["scales"][rows, :],
-                        rhs=moving["codes"][rows, c : c + MM_N].bitcast(FP8X4),
-                        rhs_scale=moving["scales"][rows, c : c + MM_N],
-                        start=True,
-                        stop=True,
-                    )
+            nc.tensor.matmul_mx(
+                out=bank[:],
+                lhsT=weights["codes"][rows, :].bitcast(FP8X4),
+                lhsT_scale=weights["scales"][rows, :],
+                rhs=moving["codes"][rows, :].bitcast(FP8X4),
+                rhs_scale=moving["scales"][rows, :],
+                start=True,
+                stop=True,
+            )
 
-        w1_op = operand("w1", M)
-        w2_op = operand("w2", M)
-        x_ops = [operand("x%d" % k, width) for k, (c0, width) in enumerate(CHUNKS)]
-        dx_ops = [operand("dx%d" % k, width) for k, (c0, width) in enumerate(CHUNKS)]
-        z_banks = [psum.tile([P, BANK], F32, name="z%d" % g) for g in range(G)]
-        tz_banks = [psum.tile([P, BANK], F32, name="tz%d" % g) for g in range(G)]
+        w1_op = operand("w1", w1, [(0, M)])
+        w2_op = operand("w2", w2, [(0, M)])
+        x_op = operand("x", x, X_PIECES)
+        dx_op = operand("dx", dx, DX_PIECES)
+        banks1 = [psum.tile([P, N], F32, name="bank1_%d" % g) for g in range(G)]
+        banks2 = [psum.tile([P, N], F32, name="bank2_%d" % g) for g in range(G)]
 
-        def per_chunk(name, parts):
-            return [sb.tile([P, G, parts * width], F32, name="%s%d" % (name, k)) for k, (c0, width) in enumerate(CHUNKS)]
+        def per_group(name):
+            return [sb.tile([P, N], F32, name="%s%d" % (name, g)) for g in range(G)]
 
-        squares = per_chunk("squares", 2)
-        z1 = per_chunk("z1", 1)
-        term1 = per_chunk("term1", 1)
-        z12 = per_chunk("z12", 1)
-        term2 = per_chunk("term2", 1)
-        sumsq = sb.tile([P, G, N], F32)
-        numer = sb.tile([P, G, N], F32)
-        logs = sb.tile([P, G, N], F32)
-        inv_cube = sb.tile([P, G, N], F32)
-        xh = sb.tile([P, G, N], F32)
-        result = sb.tile([P, G, N], F32)
-        base_sb = sb.tile([P, G, N], F32)
+        z1 = per_group("z1")
+        z1_sq = per_group("z1_sq")
+        z2_sq = per_group("z2_sq")
+        z12 = per_group("z12")
+        sumsq = per_group("sumsq")
+        term1 = per_group("term1")
+        term2 = per_group("term2")
+        numer = per_group("numer")
+        logs = per_group("logs")
+        inv_cube = per_group("inv_cube")
+        xh = per_group("xh")
+        result = per_group("result")
+        base_sb = per_group("base")
         params_rows = sb.tile([P, P], F32, align_bytes=64)
         params = sb.tile([P, P], F32, align_bytes=64)
         inv_ra = sb.tile([P, G], F32)
         ln_ra = sb.tile([P, G], F32)
         exp_bias = sb.tile([P, G], F32)
 
-        load(w1_op, w1, 0)
-        load(w2_op, w2, 0)
-        load(x_ops[0], x, CHUNKS[0][0])
-        load(dx_ops[0], dx, CHUNKS[0][0])
-        load(x_ops[1], x, CHUNKS[1][0])
-        load(x_ops[2], x, CHUNKS[2][0])
-        load(dx_ops[1], dx, CHUNKS[1][0])
-        load(dx_ops[2], dx, CHUNKS[2][0])
-        nc.sync.dma_start(out=base_sb[:], in_=base.rearrange("g m n -> m g n"))
-
         nc.vector.memset(params_rows[:], 0.0)
+        load(w2_op, 0)
         for r, vec in enumerate((ra, og)):
-            nc.scalar.dma_start(
+            nc.sync.dma_start(
                 out=params_rows[r:P:32, :].rearrange("q (g c) -> q g c", g=G),
                 in_=vec.rearrange("g (q c) o -> q g (c o)", c=32),
             )
+        for k in range(len(X_PIECES)):
+            load(x_op, k)
+        load(w1_op, 0)
+        for k in range(len(DX_PIECES)):
+            load(dx_op, k)
+        for g in range(G):
+            nc.sync.dma_start(out=base_sb[g][:], in_=base[g])
         ra_cols = params[:, 0:P:32]
 
-        round_on_vector(w1_op, 0, M)
+        round_on_vector(w2_op, 0, 0, M)
         nc.vector.transpose(out=params[:], in_=params_rows[:])
-        quantize(w1_op)
-        round_on_vector(w2_op, 0, M)
-        nc.vector.reciprocal(out=inv_ra[:], in_=ra_cols)
-        quantize(w2_op)
+        quantize(w2_op, 0)
         nc.scalar.activation(out=ln_ra[:], in_=ra_cols, func=ACT.Ln)
         nc.scalar.mul(out=exp_bias[:], in_=ln_ra[:], mul=-1.5)
+        last = len(X_PIECES) - 1
+        for k in range(last):
+            round_on_vector(x_op, k, 0, X_PIECES[k][1])
+            if k == 0:
+                nc.vector.reciprocal(out=inv_ra[:], in_=ra_cols)
+            quantize(x_op, k)
+        round_on_vector(x_op, last, 0, LAST_X_VECTOR_COLS)
+        round_on_scalar(x_op, last, LAST_X_VECTOR_COLS, X_PIECES[last][1])
+        round_on_scalar(w1_op, 0, 0, M)
+        quantize(x_op, last)
 
-        round_on_vector(x_ops[0], 0, x_ops[0]["width"])
-        quantize(x_ops[0])
         for g in range(G):
-            products(z_banks[g], g, x_ops[0])
-        round_on_vector(dx_ops[0], 0, dx_ops[0]["width"])
-        quantize(dx_ops[0])
+            product(banks2[g], g, w2_op, x_op)
+        quantize(w1_op, 0)
         for g in range(G):
-            products(tz_banks[g], g, dx_ops[0])
-        round_on_vector(x_ops[1], 0, x_ops[1]["width"])
+            product(banks1[g], g, w1_op, x_op)
 
-        def square_step(k, g):
-            width = CHUNKS[k][1]
-            nc.scalar.activation(out=squares[k][:, g, :], in_=z_banks[g][:, 0 : 2 * width], func=ACT.Square)
+        def dx_step(k):
+            round_on_vector(dx_op, k, 0, DX_PIECES[k][1])
+            quantize(dx_op, k)
 
-        def copy_step(k, g):
-            width = CHUNKS[k][1]
-            nc.scalar.copy(out=z1[k][:, g, :], in_=z_banks[g][:, 0:width])
+        def z_step(g):
+            nc.scalar.activation(out=z2_sq[g][:], in_=banks2[g][:], func=ACT.Square)
+            nc.scalar.activation(out=z1_sq[g][:], in_=banks1[g][:], func=ACT.Square)
+            nc.scalar.copy(out=z1[g][:], in_=banks1[g][:])
+            product(banks1[g], g, w1_op, dx_op)
 
-        def term1_step(k, g):
-            width = CHUNKS[k][1]
+        def z12_step(g):
+            nc.vector.tensor_tensor(out=z12[g][:], in0=z1[g][:], in1=banks2[g][:], op=ALU.mult)
+            product(banks2[g], g, w2_op, dx_op)
+
+        def sumsq_step(g, engine):
+            engine.tensor_tensor(out=sumsq[g][:], in0=z1_sq[g][:], in1=z2_sq[g][:], op=ALU.add)
+
+        def term1_step(g):
             nc.vector.scalar_tensor_tensor(
-                out=term1[k][:, g, :], in0=squares[k][:, g, width : 2 * width], scalar=params[:, 32 * g : 32 * g + 1],
-                in1=tz_banks[g][:, 0:width], op0=ALU.add, op1=ALU.mult,
+                out=term1[g][:], in0=z2_sq[g][:], scalar=params[:, 32 * g : 32 * g + 1], in1=banks1[g][:], op0=ALU.add, op1=ALU.mult
             )
 
-        def z12_step(k, g):
-            width = CHUNKS[k][1]
-            nc.vector.tensor_tensor(out=z12[k][:, g, :], in0=z1[k][:, g, :], in1=z_banks[g][:, width : 2 * width], op=ALU.mult)
+        def term2_step(g):
+            nc.vector.tensor_tensor(out=term2[g][:], in0=z12[g][:], in1=banks2[g][:], op=ALU.mult)
 
-        def term2_step(k, g):
-            width = CHUNKS[k][1]
-            nc.vector.tensor_tensor(out=term2[k][:, g, :], in0=z12[k][:, g, :], in1=tz_banks[g][:, width : 2 * width], op=ALU.mult)
+        def numer_step(g, engine):
+            engine.tensor_tensor(out=numer[g][:], in0=term1[g][:], in1=term2[g][:], op=ALU.subtract)
 
-        def sumsq_step(k):
-            c0, width = CHUNKS[k]
-            nc.vector.tensor_tensor(
-                out=sumsq[:, :, c0 : c0 + width], in0=squares[k][:, :, 0:width], in1=squares[k][:, :, width : 2 * width], op=ALU.add
-            )
-
-        def numer_step(k):
-            c0, width = CHUNKS[k]
-            nc.vector.tensor_tensor(out=numer[:, :, c0 : c0 + width], in0=term1[k][:], in1=term2[k][:], op=ALU.subtract)
-
-        def early_chunk(k, after_first_term):
-            for g in range(G):
-                square_step(k, g)
-                copy_step(k, g)
-                term1_step(k, g)
-                if g == 0:
-                    after_first_term()
-                else:
-                    term2_step(k, g - 1)
-                z12_step(k, g)
-                products(z_banks[g], g, x_ops[k + 1])
-            sumsq_step(k)
-            term2_step(k, G - 1)
-
-        early_chunk(0, lambda: quantize(x_ops[1]))
-        round_on_scalar(x_ops[2], 0, x_ops[2]["width"])
-        round_on_vector(dx_ops[1], 0, dx_ops[1]["width"])
-        numer_step(0)
-        quantize(dx_ops[1])
-        for g in range(G):
-            products(tz_banks[g], g, dx_ops[1])
-
-        early_chunk(1, lambda: quantize(x_ops[2]))
-        round_on_scalar(dx_ops[2], LAST_DX_VECTOR_COLS, dx_ops[2]["width"])
-        round_on_vector(dx_ops[2], 0, LAST_DX_VECTOR_COLS)
-        numer_step(1)
-        quantize(dx_ops[2])
-        for g in range(G):
-            products(tz_banks[g], g, dx_ops[2])
-
-        for g in range(G):
-            square_step(2, g)
-            term1_step(2, g)
-        sumsq_step(2)
-        for g in range(G):
-            copy_step(2, g)
-        for g in range(G):
-            nc.scalar.activation(out=logs[:, g, :], in_=sumsq[:, g, :], func=ACT.Ln, scale=inv_ra[:, g : g + 1], bias=1.0)
-        for g in range(G):
-            z12_step(2, g)
-        for g in range(G):
-            term2_step(2, g)
-        numer_step(2)
+        def log_step(g):
+            nc.scalar.activation(out=logs[g][:], in_=sumsq[g][:], func=ACT.Ln, scale=inv_ra[:, g : g + 1], bias=1.0)
 
         def xh_step(g):
-            nc.scalar.activation(out=inv_cube[:, g, :], in_=logs[:, g, :], func=ACT.Exp, scale=-1.5, bias=exp_bias[:, g : g + 1])
-            nc.vector.tensor_tensor(out=xh[:, g, :], in0=numer[:, g, :], in1=inv_cube[:, g, :], op=ALU.mult)
+            nc.scalar.activation(out=inv_cube[g][:], in_=logs[g][:], func=ACT.Exp, scale=-1.5, bias=exp_bias[:, g : g + 1])
+            nc.vector.tensor_tensor(out=xh[g][:], in0=numer[g][:], in1=inv_cube[g][:], op=ALU.mult)
+
+        def result_step(g, c0, c1):
+            nc.vector.scalar_tensor_tensor(
+                out=result[g][:, c0:c1], in0=xh[g][:, c0:c1], scalar=params[:, 32 * g + 1 : 32 * g + 2],
+                in1=base_sb[g][:, c0:c1], op0=ALU.mult, op1=ALU.add,
+            )
+            nc.sync.dma_start(out=out[g][:, c0:c1], in_=result[g][:, c0:c1])
+
+        dx_step(0)
+        dx_step(1)
+        z_step(0)
+        sumsq_step(0, nc.vector)
+        z12_step(0)
+        for g in range(1, G):
+            z_step(g)
+            sumsq_step(g, nc.gpsimd)
+            term1_step(g - 1)
+            z12_step(g)
+            term2_step(g - 1)
+        for g in range(1):
+            numer_step(g, nc.gpsimd)
+        for g in range(G):
+            log_step(g)
+        term1_step(G - 1)
+        term2_step(G - 1)
+        for g in range(1, G):
+            numer_step(g, nc.vector)
 
         xh_step(0)
-        for g in range(G):
-            if g + 1 < G:
-                xh_step(g + 1)
-            nc.vector.scalar_tensor_tensor(
-                out=result[:, g, :], in0=xh[:, g, :], scalar=params[:, 32 * g + 1 : 32 * g + 2],
-                in1=base_sb[:, g, :], op0=ALU.mult, op1=ALU.add,
-            )
-            nc.sync.dma_start(out=out[g], in_=result[:, g, :])
+        for g in range(G - 1):
+            xh_step(g + 1)
+            result_step(g, 0, N)
+        result_step(G - 1, 0, N // 2)
+        result_step(G - 1, N // 2, N)

from contextlib import ExitStack

import concourse.mybir as mybir

G, D, M, N = 4, 128, 128, 512
FLOPS = 4 * 2 * G * D * M * N

F32 = mybir.dt.float32
BF16 = mybir.dt.bfloat16
U32 = mybir.dt.uint32
U8 = mybir.dt.uint8
FP8X4 = mybir.dt.float8_e4m3fn_x4
ACT = mybir.ActivationFunctionType
ALU = mybir.AluOpType

P = 128
PACK = 4
ROWS = D // PACK
RUN = 4
X_PIECES = [(0, 256), (256, 256)]
DX_PIECES = [(0, 256), (256, 256)]
LAST_X_VECTOR_COLS = 160


def tile_rows_tnsphere_kernel(tc, x, w1, w2, ra, dx, og, base, out):
    nc = tc.nc

    with ExitStack() as ctx:
        sb = ctx.enter_context(tc.tile_pool(name="sb", bufs=1))
        psum = ctx.enter_context(tc.psum_pool(name="psum", bufs=1))
        ctx.enter_context(tc.manual_schedule())

        def operand(name, src, pieces):
            width = sum(w for c0, w in pieces)
            return {
                "rows": src.rearrange("g (p j) n -> (g p) j n", j=PACK),
                "pieces": pieces,
                "raw": [sb.tile([P, PACK, w], F32, name="%s_raw%d" % (name, c0), align_bytes=64) for c0, w in pieces],
                "rounded": [sb.tile([P, w * PACK], BF16, name="%s_rounded%d" % (name, c0), align_bytes=64) for c0, w in pieces],
                "codes": sb.tile([P, width], U32, name=name + "_codes", align_bytes=64),
                "scales": sb.tile([P, width], U8, name=name + "_scales", align_bytes=64),
            }

        def load(op, k):
            c0, w = op["pieces"][k]
            nc.sync.dma_start(out=op["raw"][k][:], in_=op["rows"][:, :, c0 : c0 + w])

        def round_views(op, k, c0, c1):
            dst = op["rounded"][k][:, c0 * PACK : c1 * PACK].rearrange("p (c i j) -> p c j i", i=RUN, j=PACK)
            src = op["raw"][k][:, :, c0:c1].rearrange("p j (c i) -> p c j i", i=RUN)
            return dst, src

        def round_on_vector(op, k, c0, c1):
            dst, src = round_views(op, k, c0, c1)
            nc.vector.tensor_copy(out=dst, in_=src)

        def round_on_scalar(op, k, c0, c1):
            dst, src = round_views(op, k, c0, c1)
            nc.scalar.copy(out=dst, in_=src)

        def quantize(op, k):
            c0, w = op["pieces"][k]
            nc.vector.quantize_mx(
                out=op["codes"][:, c0 : c0 + w].bitcast(FP8X4), scales=op["scales"][:, c0 : c0 + w], in_=op["rounded"][k][:]
            )

        def product(bank, g, weights, moving):
            rows = slice(ROWS * g, ROWS * (g + 1))
            nc.tensor.matmul_mx(
                out=bank[:],
                lhsT=weights["codes"][rows, :].bitcast(FP8X4),
                lhsT_scale=weights["scales"][rows, :],
                rhs=moving["codes"][rows, :].bitcast(FP8X4),
                rhs_scale=moving["scales"][rows, :],
                start=True,
                stop=True,
            )

        w1_op = operand("w1", w1, [(0, M)])
        w2_op = operand("w2", w2, [(0, M)])
        x_op = operand("x", x, X_PIECES)
        dx_op = operand("dx", dx, DX_PIECES)
        banks1 = [psum.tile([P, N], F32, name="bank1_%d" % g) for g in range(G)]
        banks2 = [psum.tile([P, N], F32, name="bank2_%d" % g) for g in range(G)]

        def per_group(name):
            return [sb.tile([P, N], F32, name="%s%d" % (name, g)) for g in range(G)]

        z1 = per_group("z1")
        z1_sq = per_group("z1_sq")
        z2_sq = per_group("z2_sq")
        z12 = per_group("z12")
        sumsq = per_group("sumsq")
        term1 = per_group("term1")
        term2 = per_group("term2")
        numer = per_group("numer")
        logs = per_group("logs")
        inv_cube = per_group("inv_cube")
        xh = per_group("xh")
        result = per_group("result")
        base_sb = per_group("base")
        params_rows = sb.tile([P, P], F32, align_bytes=64)
        params = sb.tile([P, P], F32, align_bytes=64)
        inv_ra = sb.tile([P, G], F32)
        ln_ra = sb.tile([P, G], F32)
        exp_bias = sb.tile([P, G], F32)

        nc.vector.memset(params_rows[:], 0.0)
        load(w2_op, 0)
        for r, vec in enumerate((ra, og)):
            nc.sync.dma_start(
                out=params_rows[r:P:32, :].rearrange("q (g c) -> q g c", g=G),
                in_=vec.rearrange("g (q c) o -> q g (c o)", c=32),
            )
        for k in range(len(X_PIECES)):
            load(x_op, k)
        load(w1_op, 0)
        for k in range(len(DX_PIECES)):
            load(dx_op, k)
        for g in range(G):
            nc.sync.dma_start(out=base_sb[g][:], in_=base[g])
        ra_cols = params[:, 0:P:32]

        round_on_vector(w2_op, 0, 0, M)
        nc.vector.transpose(out=params[:], in_=params_rows[:])
        quantize(w2_op, 0)
        nc.scalar.activation(out=ln_ra[:], in_=ra_cols, func=ACT.Ln)
        nc.scalar.mul(out=exp_bias[:], in_=ln_ra[:], mul=-1.5)
        last = len(X_PIECES) - 1
        for k in range(last):
            round_on_vector(x_op, k, 0, X_PIECES[k][1])
            if k == 0:
                nc.vector.reciprocal(out=inv_ra[:], in_=ra_cols)
            quantize(x_op, k)
        round_on_vector(x_op, last, 0, LAST_X_VECTOR_COLS)
        round_on_scalar(x_op, last, LAST_X_VECTOR_COLS, X_PIECES[last][1])
        round_on_scalar(w1_op, 0, 0, M)
        quantize(x_op, last)

        for g in range(G):
            product(banks2[g], g, w2_op, x_op)
        quantize(w1_op, 0)
        for g in range(G):
            product(banks1[g], g, w1_op, x_op)

        def dx_step(k):
            round_on_vector(dx_op, k, 0, DX_PIECES[k][1])
            quantize(dx_op, k)

        def z_step(g):
            nc.scalar.activation(out=z2_sq[g][:], in_=banks2[g][:], func=ACT.Square)
            nc.scalar.activation(out=z1_sq[g][:], in_=banks1[g][:], func=ACT.Square)
            nc.scalar.copy(out=z1[g][:], in_=banks1[g][:])
            product(banks1[g], g, w1_op, dx_op)

        def z12_step(g):
            nc.vector.tensor_tensor(out=z12[g][:], in0=z1[g][:], in1=banks2[g][:], op=ALU.mult)
            product(banks2[g], g, w2_op, dx_op)

        def sumsq_step(g, engine):
            engine.tensor_tensor(out=sumsq[g][:], in0=z1_sq[g][:], in1=z2_sq[g][:], op=ALU.add)

        def term1_step(g):
            nc.vector.scalar_tensor_tensor(
                out=term1[g][:], in0=z2_sq[g][:], scalar=params[:, 32 * g : 32 * g + 1], in1=banks1[g][:], op0=ALU.add, op1=ALU.mult
            )

        def term2_step(g):
            nc.vector.tensor_tensor(out=term2[g][:], in0=z12[g][:], in1=banks2[g][:], op=ALU.mult)

        def numer_step(g, engine):
            engine.tensor_tensor(out=numer[g][:], in0=term1[g][:], in1=term2[g][:], op=ALU.subtract)

        def log_step(g):
            nc.scalar.activation(out=logs[g][:], in_=sumsq[g][:], func=ACT.Ln, scale=inv_ra[:, g : g + 1], bias=1.0)

        def xh_step(g):
            nc.scalar.activation(out=inv_cube[g][:], in_=logs[g][:], func=ACT.Exp, scale=-1.5, bias=exp_bias[:, g : g + 1])
            nc.vector.tensor_tensor(out=xh[g][:], in0=numer[g][:], in1=inv_cube[g][:], op=ALU.mult)

        def result_step(g, c0, c1):
            nc.vector.scalar_tensor_tensor(
                out=result[g][:, c0:c1], in0=xh[g][:, c0:c1], scalar=params[:, 32 * g + 1 : 32 * g + 2],
                in1=base_sb[g][:, c0:c1], op0=ALU.mult, op1=ALU.add,
            )
            nc.sync.dma_start(out=out[g][:, c0:c1], in_=result[g][:, c0:c1])

        dx_step(0)
        dx_step(1)
        z_step(0)
        sumsq_step(0, nc.vector)
        z12_step(0)
        for g in range(1, G):
            z_step(g)
            sumsq_step(g, nc.gpsimd)
            term1_step(g - 1)
            z12_step(g)
            term2_step(g - 1)
        for g in range(1):
            numer_step(g, nc.gpsimd)
        for g in range(G):
            log_step(g)
        term1_step(G - 1)
        term2_step(G - 1)
        for g in range(1, G):
            numer_step(g, nc.vector)

        xh_step(0)
        for g in range(G - 1):
            xh_step(g + 1)
            result_step(g, 0, N)
        result_step(G - 1, 0, N // 2)
        result_step(G - 1, N // 2, N)
